import numpy as np
import ml_dtypes


def mxq(x, axis, fmt="e4m3"):
    dtype, down = {"e4m3": (ml_dtypes.float8_e4m3fn, 7), "e5m2": (ml_dtypes.float8_e5m2, 14)}[fmt]
    v = np.moveaxis(np.asarray(x, np.float32).astype(ml_dtypes.bfloat16).astype(np.float64), axis, -1)
    blocks = v.reshape(v.shape[:-1] + (-1, 32))
    amax = np.abs(blocks).max(-1, keepdims=True)
    byte = np.maximum(np.where(amax > 0, np.frexp(amax)[1] - 1 + 127, 0) - down, 1)
    scale = np.exp2(byte - 127.0)
    codes = (blocks / scale).astype(np.float32).astype(dtype).astype(np.float64)
    return np.moveaxis((codes * scale).reshape(v.shape), -1, axis)


WIDE = False


def mx_kscale(k):
    if not WIDE:
        return np.ones(k)
    levels = np.array([10, -10, 5, -5, 0])
    if k % 512:
        return np.exp2(np.random.permutation(np.resize(levels, k // 32))).repeat(32)
    a = np.empty((k // 512, 16))
    for p in range(k // 512):
        a[p, :8] = np.random.permutation(np.resize(levels, 8))
        for g in range(8):
            far = levels[np.abs(levels - a[p, g]) >= 10]
            a[p, g + 8] = far[np.random.randint(len(far))]
    return np.exp2(a.ravel()).repeat(32)


BF16 = ml_dtypes.bfloat16


def bf(x):
    return np.asarray(x, np.float32).astype(BF16)


def f64(x):
    return np.asarray(x).astype(np.float64)

def planes(Y):
    n, m = Y.shape
    b = f64(bf(Y)).reshape(n // 32, 32, m)
    amax = np.abs(b).max(1)
    byte = np.clip(np.where(amax > 0, np.frexp(amax)[1] - 1 + 127 - 7, 1), 1, 254)
    codes = (b * np.exp2(127.0 - byte)[:, None, :]).reshape(n, m).astype(np.float32).astype(ml_dtypes.float8_e4m3fn).view(np.uint8)
    words = codes.reshape(n // 512, 128, 4, m).transpose(0, 1, 3, 2)
    return np.ascontiguousarray(words), np.ascontiguousarray(byte.astype(np.uint8).reshape(n // 512, 16, m))


V, K, P, R = 1024, 512, 768, 2048


def setup_inputs():
    s1, s2 = mx_kscale(V), mx_kscale(V)
    t = mx_kscale(K)
    return {
        "psi1": bf(np.random.standard_normal((V, K)) / np.sqrt(V) * s1[:, None]),
        "x1": bf(np.random.standard_normal((V, P)) / s1[:, None]),
        "psi2": bf(np.random.standard_normal((V, K)) / np.sqrt(V) * s2[:, None]),
        "x2": bf(np.random.standard_normal((V, P)) / s2[:, None]),
        "lam": bf(np.random.uniform(0.0, 2.0, K)),
        "g": bf((1.0 + 0.1 * np.random.standard_normal(K)) * t),
        "phi3": bf(np.random.standard_normal((R, K)) / np.sqrt(K) / t[None, :]),
    }


def analyze(psi, x):
    return mxq(f64(psi), 0, "e4m3").T @ mxq(f64(x), 0, "e4m3")


def low_pass_weight(lam):
    return 1.0 / (1.0 + np.exp(-4.0 * (1.0 - lam)))


def core(psi1, x1, psi2, x2, lam, g, phi3):
    c1 = analyze(psi1, x1)
    c2 = analyze(psi2, x2)
    h = low_pass_weight(f64(lam))[:, None]
    c = h * c1 + (1.0 - h) * c2
    cg = f64(g)[:, None] * c
    return mxq(f64(phi3), 1, "e4m3") @ mxq(cg, 0, "e4m3")


def reference(psi1, x1, psi2, x2, lam, g, phi3):
    R_out = core(psi1, x1, psi2, x2, lam, g, phi3)
    words, scales = planes(R_out)
    return R_out, words, scales

@@ -1,0 +1,423 @@
+from contextlib import ExitStack
+
+import concourse.mybir as mybir
+from concourse.masks import make_identity
+
+F32 = mybir.dt.float32
+BF16 = mybir.dt.bfloat16
+I32 = mybir.dt.int32
+U32 = mybir.dt.uint32
+U8 = mybir.dt.uint8
+FP8X4 = mybir.dt.float8_e4m3fn_x4
+ALU = mybir.AluOpType
+ACT = mybir.ActivationFunctionType
+
+V, K, N, R = 1024, 512, 768, 2048
+P = 128
+G = R // 512
+CH = ((0, 256), (256, 512), (512, 768))
+FLOPS = 2 * (2 * V * K * N + R * K * N)
+
+
+def tile_coupledbasisspectralposetransfer_x1_kernel(
+    tc, psi1, x1, psi2, x2, lam, g, phi3, out_0, out_1, out_2
+):
+    nc = tc.nc
+    psi_in = (psi1, psi2)
+    x_in = (x1, x2)
+
+    with ExitStack() as ctx:
+        keep = ctx.enter_context(tc.tile_pool(name="keep", bufs=1))
+        work = ctx.enter_context(tc.tile_pool(name="work", bufs=2))
+        psum = ctx.enter_context(tc.psum_pool(name="psum", bufs=8))
+        ctx.enter_context(tc.manual_schedule())
+
+        def kept(shape, dtype, name):
+            return keep.tile(shape, dtype, name=name, align_bytes=64)
+
+        lam_t = kept([P, 4], BF16, "lam_t")
+        g_t = kept([P, 4], BF16, "g_t")
+        nc.scalar.dma_start(out=lam_t[:], in_=lam.rearrange("(p t) -> p t", t=4))
+        nc.scalar.dma_start(out=g_t[:], in_=g.rearrange("(p t) -> p t", t=4))
+
+        psi_raw = {}
+        x_raw = {}
+        for b in range(2):
+            for q in range(2):
+                rows = slice(512 * q, 512 * q + 512)
+                psi_raw[b, q] = kept([P, 4, K], BF16, "psi_raw_%d%d" % (b, q))
+                nc.sync.dma_start(
+                    out=psi_raw[b, q][:], in_=psi_in[b][rows, :].rearrange("(p j) c -> p j c", j=4)
+                )
+                x_raw[b, q] = kept([P, 4, N], BF16, "x_raw_%d%d" % (b, q))
+                nc.sync.dma_start(
+                    out=x_raw[b, q][:], in_=x_in[b][rows, :].rearrange("(p j) c -> p j c", j=4)
+                )
+        phi_raw = {}
+        for gg in range(G):
+            phi_raw[gg] = kept([P, 4, K], BF16, "phi_raw_%d" % gg)
+            nc.sync.dma_start(
+                out=phi_raw[gg][:],
+                in_=phi3[512 * gg : 512 * gg + 512, :].rearrange("(p t) k -> p t k", t=4),
+            )
+
+        ident = kept([P, P], F32, "ident")
+        make_identity(nc, ident[:])
+
+        arg = kept([P, 4], F32, "arg")
+        nc.vector.tensor_scalar(
+            out=arg[:], in0=lam_t[:], scalar1=4.0, scalar2=-4.0, op0=ALU.mult, op1=ALU.add
+        )
+        ex = kept([P, 4], F32, "ex")
+        nc.scalar.activation(out=ex[:], in_=arg[:], func=ACT.Exp)
+        den = kept([P, 4], F32, "den")
+        nc.vector.tensor_scalar_add(den[:], ex[:], 1.0)
+        h = kept([P, 4], F32, "h")
+        nc.vector.reciprocal(h[:], den[:])
+        hm = kept([P, 4], F32, "hm")
+        nc.vector.tensor_scalar(out=hm[:], in0=h[:], scalar1=-1.0, scalar2=1.0, op0=ALU.mult, op1=ALU.add)
+        a1 = kept([P, 4], F32, "a1")
+        nc.vector.tensor_tensor(out=a1[:], in0=h[:], in1=g_t[:], op=ALU.mult)
+        a2 = kept([P, 4], F32, "a2")
+        nc.vector.tensor_tensor(out=a2[:], in0=hm[:], in1=g_t[:], op=ALU.mult)
+
+        psi_grp = {}
+        x_grp = {}
+        psi_c, psi_s, x_c, x_s = {}, {}, {}, {}
+        for b in range(2):
+            for q in range(2):
+                tag = "%d%d" % (b, q)
+                psi_grp[b, q] = kept([P, 4, P, 4], BF16, "psi_grp_" + tag)
+                x_grp[b, q] = kept([P, N, 4], BF16, "x_grp_" + tag)
+                psi_c[b, q] = kept([P, K], U32, "psi_c_" + tag)
+                psi_s[b, q] = kept([P, K], U8, "psi_s_" + tag)
+                x_c[b, q] = kept([P, N], U32, "x_c_" + tag)
+                x_s[b, q] = kept([P, N], U8, "x_s_" + tag)
+        phi_grp, phi_c, phi_s = {}, {}, {}
+        for gg in range(G):
+            phi_grp[gg] = kept([P, 4, P, 4], BF16, "phi_grp_%d" % gg)
+            phi_c[gg] = kept([P, K], U32, "phi_c_%d" % gg)
+            phi_s[gg] = kept([P, K], U8, "phi_s_%d" % gg)
+        part1 = kept([P, 4, N], F32, "part1")
+        cg_flat, cg_grp, cg_c, cg_s = {}, {}, {}, {}
+        for ch in CH:
+            w = ch[1] - ch[0]
+            cg_flat[ch] = kept([P, 4, w], BF16, "cg_flat_%d" % ch[0])
+            cg_grp[ch] = kept([P, w, 4], BF16, "cg_grp_%d" % ch[0])
+            cg_c[ch] = kept([P, w], U32, "cg_c_%d" % ch[0])
+            cg_s[ch] = kept([P, w], U8, "cg_s_%d" % ch[0])
+        out_s = kept([P, G, N], U8, "out_s")
+
+        def copy(eng, dst, src):
+            if eng == "v":
+                nc.vector.tensor_copy(out=dst, in_=src)
+            else:
+                nc.scalar.copy(out=dst, in_=src)
+
+        def quant(codes, scales, src):
+            nc.vector.quantize_mx(out=codes.bitcast(FP8X4), scales=scales, in_=src)
+
+        def interleave(eng, dst, src):
+            copy(
+                eng,
+                dst.rearrange("p (c i) t -> p c t i", i=4),
+                src.rearrange("p t (c i) -> p c t i", i=4),
+            )
+
+        def i_psi(eng, b, q, t0, t1):
+            src = psi_raw[b, q][:].rearrange("p j (m t) -> p t m j", t=4)
+            copy(eng, psi_grp[b, q][:, t0:t1], src[:, t0:t1])
+
+        def q_psi(b, q):
+            quant(psi_c[b, q][:], psi_s[b, q][:], psi_grp[b, q][:].rearrange("p t m j -> p (t m j)"))
+
+        def i_x(eng, b, q, a, z):
+            interleave(eng, x_grp[b, q][:, a:z, :], x_raw[b, q][:, :, a:z])
+
+        def q_x(b, q, a, z):
+            quant(
+                x_c[b, q][:, a:z],
+                x_s[b, q][:, a:z],
+                x_grp[b, q][:, a:z, :].rearrange("p n j -> p (n j)"),
+            )
+
+        def mm(dst, lc, ls, m, rc, rs, n0, n1, start, stop):
+            nc.tensor.matmul_mx(
+                out=dst,
+                lhsT=lc[:, m : m + P].bitcast(FP8X4),
+                lhsT_scale=ls[:, m : m + P],
+                rhs=rc[:, n0:n1].bitcast(FP8X4),
+                rhs_scale=rs[:, n0:n1],
+                start=start,
+                stop=stop,
+            )
+
+        bank = {}
+
+        def mm1(b, ch, ts):
+            w = ch[1] - ch[0]
+            acc = psum.tile([P, len(ts), w], F32, name="acc1", tag="bank")
+            bank[b, ch, ts] = acc
+            for i in range(len(ts)):
+                for q in range(2):
+                    mm(
+                        acc[:, i, :], psi_c[b, q], psi_s[b, q], P * ts[i],
+                        x_c[b, q], x_s[b, q], ch[0], ch[1], q == 0, q == 1,
+                    )
+
+        def scale1(ch, ts):
+            for i in range(len(ts)):
+                t = ts[i]
+                nc.scalar.activation(
+                    out=part1[:, t, ch[0] : ch[1]], in_=bank[0, ch, ts][:, i, :],
+                    func=ACT.Copy, scale=a1[:, t : t + 1],
+                )
+
+        def blend(ch, ts):
+            for i in range(len(ts)):
+                t = ts[i]
+                nc.vector.scalar_tensor_tensor(
+                    out=cg_flat[ch][:, t, :], in0=bank[1, ch, ts][:, i, :], scalar=a2[:, t : t + 1],
+                    in1=part1[:, t, ch[0] : ch[1]], op0=ALU.mult, op1=ALU.add,
+                )
+
+        def i_cg(ch):
+            interleave("v", cg_grp[ch][:], cg_flat[ch][:])
+
+        def q_cg(ch):
+            quant(cg_c[ch][:], cg_s[ch][:], cg_grp[ch][:].rearrange("p n j -> p (n j)"))
+
+        def t_phi(gg):
+            words = phi_raw[gg][:].rearrange("p t k -> p (t k)").bitcast(F32)
+            for half in range(2):
+                acc = psum.tile([P, 2, 2, P], F32, name="acct", tag="bank")
+                bank["phi", gg, half] = acc
+                for a in range(2):
+                    t = 2 * half + a
+                    for u in range(2):
+                        nc.tensor.transpose(acc[:, a, u, :], words[:, 256 * t + u : 256 * (t + 1) : 2], ident[:])
+
+        def c_phi(eng, gg, half):
+            dst = phi_grp[gg][:, 2 * half : 2 * half + 2].rearrange("p a m j -> p (a m j)").bitcast(F32)
+            copy(
+                eng,
+                dst.rearrange("p (a m u) -> p a m u", a=2, u=2),
+                bank["phi", gg, half][:].rearrange("p a u m -> p a m u"),
+            )
+
+        def q_phi(gg):
+            quant(phi_c[gg][:], phi_s[gg][:], phi_grp[gg][:].rearrange("p t m j -> p (t m j)"))
+
+        out_f, out_b, out_c = {}, {}, {}
+
+        def mm2(gg, ch):
+            w = ch[1] - ch[0]
+            per = 512 // w
+            for i in range(4 // per):
+                acc = psum.tile([P, per, w], F32, name="acc2", tag="bank")
+                bank["out", gg, ch, i] = acc
+                for k in range(per):
+                    mm(
+                        acc[:, k, :], phi_c[gg], phi_s[gg], P * (per * i + k),
+                        cg_c[ch], cg_s[ch], 0, w, True, True,
+                    )
+
+        def empty(gg, ch, engines):
+            w = ch[1] - ch[0]
+            per = 512 // w
+            out_f[gg, ch] = work.tile([P, 4, w], F32, name="out_f", bufs=6, align_bytes=64)
+            for i in range(4 // per):
+                copy(engines[i], out_f[gg, ch][:, per * i : per * i + per, :], bank["out", gg, ch, i][:])
+
+        def store_f(gg, ch, a, z):
+            nc.sync.dma_start(
+                out=out_0[512 * gg : 512 * gg + 512, ch[0] + a : ch[0] + z].rearrange("(p t) n -> p t n", t=4),
+                in_=out_f[gg, ch][:, :, a:z],
+            )
+
+        def round_out(gg, ch, a, z):
+            if a == 0:
+                w = ch[1] - ch[0]
+                out_b[gg, ch] = work.tile([P, w, 4], BF16, name="out_b", bufs=4, align_bytes=64)
+                out_c[gg, ch] = work.tile([P, w], U32, name="out_c", bufs=6, align_bytes=64)
+            interleave("v", out_b[gg, ch][:, a:z, :], out_f[gg, ch][:, :, a:z])
+
+        def q_out(gg, ch, a, z):
+            quant(
+                out_c[gg, ch][:, a:z], out_s[:, gg, ch[0] + a : ch[0] + z],
+                out_b[gg, ch][:, a:z, :].rearrange("p n j -> p (n j)"),
+            )
+            nc.sync.dma_start(
+                out=out_1[gg, :, ch[0] + a : ch[0] + z, :].rearrange("p n t -> p (n t)").bitcast(I32),
+                in_=out_c[gg, ch][:, a:z].bitcast(I32),
+            )
+
+        def store_s(g0, g1, a, z):
+            for quad in range(4):
+                nc.sync.dma_start(
+                    out=out_2[g0:g1, 4 * quad : 4 * quad + 4, a:z].bitcast(I32).rearrange("g q n -> q g n"),
+                    in_=out_s[32 * quad : 32 * quad + 4, g0:g1, a:z].bitcast(I32),
+                )
+
+        T01, T23 = (0, 1), (2, 3)
+
+        def xi(eng, b, q, c):
+            i_x(eng, b, q, 256 * c, 256 * c + 256)
+
+        def xq(b, q, c):
+            q_x(b, q, 256 * c, 256 * c + 256)
+
+        def m1(b, c, h):
+            mm1(b, CH[c], (T01, T23)[h])
+
+        def sc(c, h):
+            scale1(CH[c], (T01, T23)[h])
+
+        def bl(c, h):
+            blend(CH[c], (T01, T23)[h])
+
+        def m2(gg, c):
+            mm2(gg, CH[c])
+
+        def A(gg, c, engines):
+            empty(gg, CH[c], engines)
+            store_f(gg, CH[c], 0, 256)
+
+        def B(gg, c):
+            round_out(gg, CH[c], 0, 256)
+
+        def Q(gg, c):
+            q_out(gg, CH[c], 0, 256)
+
+        xi("s", 0, 0, 2)
+        i_psi("v", 0, 0, 2, 4)
+        xi("v", 0, 0, 1)
+        t_phi(0)
+        i_psi("v", 0, 0, 0, 2)
+        i_psi("v", 0, 1, 0, 2)
+        xq(0, 0, 1)
+        q_psi(0, 0)
+        i_psi("s", 0, 1, 2, 4)
+        xi("v", 0, 1, 1)
+        xi("s", 0, 0, 0)
+        i_psi("s", 1, 0, 2, 4)
+        xi("s", 0, 1, 2)
+        q_psi(0, 1)
+        xq(0, 0, 2)
+        i_psi("s", 1, 1, 2, 4)
+        t_phi(1)
+        xi("s", 1, 0, 2)
+        xi("s", 1, 1, 2)
+        c_phi("s", 0, 0)
+        xq(0, 1, 1)
+        i_psi("v", 1, 0, 0, 2)
+        xi("v", 1, 0, 1)
+        xi("v", 1, 0, 0)
+        m1(0, 1, 1)
+        c_phi("s", 0, 1)
+        i_psi("v", 1, 1, 0, 2)
+        xq(0, 1, 2)
+        xi("v", 0, 1, 0)
+        xq(0, 0, 0)
+        q_psi(1, 1)
+        xq(0, 1, 0)
+        xi("v", 1, 1, 0)
+        q_psi(1, 0)
+        xq(1, 0, 1)
+        xq(1, 1, 0)
+        xq(1, 0, 2)
+        m1(0, 0, 1)
+        xq(1, 1, 2)
+        xq(1, 0, 0)
+        m1(0, 0, 0)
+        xi("v", 1, 1, 1)
+        m1(1, 0, 0)
+        m1(1, 0, 1)
+        m1(0, 1, 0)
+        c_phi("s", 1, 0)
+        c_phi("s", 1, 1)
+        sc(1, 1)
+        sc(0, 0)
+        sc(0, 1)
+        t_phi(3)
+        q_phi(0)
+        t_phi(2)
+        sc(1, 0)
+        bl(0, 0)
+        bl(0, 1)
+        c_phi("s", 3, 1)
+        xq(1, 1, 1)
+        i_cg(CH[0])
+        q_phi(1)
+        c_phi("s", 3, 0)
+        c_phi("s", 2, 1)
+        q_cg(CH[0])
+        c_phi("v", 2, 0)
+        m1(0, 2, 0)
+        q_phi(3)
+        m2(0, 0)
+        q_phi(2)
+        m1(1, 1, 1)
+        bl(1, 1)
+        m1(1, 1, 0)
+        bl(1, 0)
+        sc(2, 0)
+        m2(2, 0)
+        A(0, 0, "ss")
+        B(0, 0)
+        i_cg(CH[1])
+        A(2, 0, "ss")
+        B(2, 0)
+        m1(1, 2, 0)
+        q_cg(CH[1])
+        bl(2, 0)
+        m2(3, 0)
+        m2(1, 0)
+        A(3, 0, "ss")
+        m1(1, 2, 1)
+        m1(0, 2, 1)
+        m2(3, 1)
+        A(1, 0, "ss")
+        Q(0, 0)
+        sc(2, 1)
+        B(1, 0)
+        Q(2, 0)
+        Q(1, 0)
+        bl(2, 1)
+        A(3, 1, "ss")
+        B(3, 0)
+        m2(1, 1)
+        A(1, 1, "ss")
+        m2(2, 1)
+        i_cg(CH[2])
+        Q(3, 0)
+        A(2, 1, "ss")
+        m2(0, 1)
+        q_cg(CH[2])
+        m2(2, 2)
+        A(0, 1, "ss")
+        m2(3, 2)
+        B(3, 1)
+        B(2, 1)
+        m2(1, 2)
+        B(1, 1)
+        Q(3, 1)
+        Q(2, 1)
+        A(2, 2, "ss")
+        B(0, 1)
+        Q(1, 1)
+        A(3, 2, "ss")
+        B(2, 2)
+        m2(0, 2)
+        A(1, 2, "vv")
+        Q(0, 1)
+        store_s(0, 4, 0, 512)
+        B(1, 2)
+        B(3, 2)
+        Q(1, 2)
+        A(0, 2, "ss")
+        Q(3, 2)
+        B(0, 2)
+        Q(2, 2)
+        Q(0, 2)
+        store_s(0, 4, 512, 768)

@@ -40,22 +40,27 @@ def tile_coupledbasisspectralposetransfer_x1_kernel(
         nc.scalar.dma_start(out=lam_t[:], in_=lam.rearrange("(p t) -> p t", t=4))
         nc.scalar.dma_start(out=g_t[:], in_=g.rearrange("(p t) -> p t", t=4))
 
-        psi_raw = {}
-        x_raw = {}
+        psi_raw, x_raw, phi_raw = {}, {}, {}
         for b in range(2):
             for q in range(2):
-                rows = slice(512 * q, 512 * q + 512)
                 psi_raw[b, q] = kept([P, 4, K], BF16, "psi_raw_%d%d" % (b, q))
-                nc.sync.dma_start(
-                    out=psi_raw[b, q][:], in_=psi_in[b][rows, :].rearrange("(p j) c -> p j c", j=4)
-                )
                 x_raw[b, q] = kept([P, 4, N], BF16, "x_raw_%d%d" % (b, q))
-                nc.sync.dma_start(
-                    out=x_raw[b, q][:], in_=x_in[b][rows, :].rearrange("(p j) c -> p j c", j=4)
-                )
-        phi_raw = {}
         for gg in range(G):
             phi_raw[gg] = kept([P, 4, K], BF16, "phi_raw_%d" % gg)
+
+        def load_psi(b, q):
+            nc.sync.dma_start(
+                out=psi_raw[b, q][:],
+                in_=psi_in[b][512 * q : 512 * q + 512, :].rearrange("(p j) c -> p j c", j=4),
+            )
+
+        def load_x(b, q):
+            nc.sync.dma_start(
+                out=x_raw[b, q][:],
+                in_=x_in[b][512 * q : 512 * q + 512, :].rearrange("(p j) c -> p j c", j=4),
+            )
+
+        def load_phi(gg):
             nc.sync.dma_start(
                 out=phi_raw[gg][:],
                 in_=phi3[512 * gg : 512 * gg + 512, :].rearrange("(p t) k -> p t k", t=4),
@@ -289,135 +294,147 @@ def tile_coupledbasisspectralposetransfer_x1_kernel(
         def Q(gg, c):
             q_out(gg, CH[c], 0, 256)
 
-        xi("s", 0, 0, 2)
+        load_psi(0, 0)
         i_psi("v", 0, 0, 2, 4)
-        xi("v", 0, 0, 1)
-        t_phi(0)
-        i_psi("v", 0, 0, 0, 2)
+        i_psi("s", 0, 0, 0, 2)
+        load_psi(0, 1)
         i_psi("v", 0, 1, 0, 2)
-        xq(0, 0, 1)
-        q_psi(0, 0)
         i_psi("s", 0, 1, 2, 4)
-        xi("v", 0, 1, 1)
-        xi("s", 0, 0, 0)
-        i_psi("s", 1, 0, 2, 4)
-        xi("s", 0, 1, 2)
         q_psi(0, 1)
-        xq(0, 0, 2)
-        i_psi("s", 1, 1, 2, 4)
-        t_phi(1)
-        xi("s", 1, 0, 2)
-        xi("s", 1, 1, 2)
-        c_phi("s", 0, 0)
-        xq(0, 1, 1)
-        i_psi("v", 1, 0, 0, 2)
-        xi("v", 1, 0, 1)
-        xi("v", 1, 0, 0)
-        m1(0, 1, 1)
-        c_phi("s", 0, 1)
-        i_psi("v", 1, 1, 0, 2)
+        load_x(0, 1)
+        xi("v", 0, 1, 2)
+        load_x(0, 0)
+        load_psi(1, 0)
+        q_psi(0, 0)
         xq(0, 1, 2)
-        xi("v", 0, 1, 0)
-        xq(0, 0, 0)
-        q_psi(1, 1)
+        xi("s", 0, 1, 1)
+        load_x(1, 1)
+        xi("v", 0, 0, 2)
+        xi("s", 0, 1, 0)
+        i_psi("v", 1, 0, 2, 4)
+        load_psi(1, 1)
+        i_psi("v", 1, 0, 0, 2)
         xq(0, 1, 0)
-        xi("v", 1, 1, 0)
+        xi("s", 0, 0, 1)
+        load_x(1, 0)
+        xq(0, 1, 1)
         q_psi(1, 0)
-        xq(1, 0, 1)
-        xq(1, 1, 0)
-        xq(1, 0, 2)
+        load_phi(0)
+        xi("s", 0, 0, 0)
+        xq(0, 0, 2)
+        xq(0, 0, 0)
+        i_psi("v", 1, 1, 2, 4)
+        xi("s", 1, 1, 0)
+        xi("v", 1, 1, 2)
+        load_phi(3)
+        xi("v", 1, 0, 0)
         m1(0, 0, 1)
-        xq(1, 1, 2)
+        xq(1, 1, 0)
+        load_phi(2)
+        i_psi("s", 1, 1, 0, 2)
+        sc(0, 1)
         xq(1, 0, 0)
         m1(0, 0, 0)
-        xi("v", 1, 1, 1)
-        m1(1, 0, 0)
-        m1(1, 0, 1)
-        m1(0, 1, 0)
-        c_phi("s", 1, 0)
-        c_phi("s", 1, 1)
-        sc(1, 1)
+        q_psi(1, 1)
+        t_phi(0)
         sc(0, 0)
-        sc(0, 1)
-        t_phi(3)
-        q_phi(0)
-        t_phi(2)
-        sc(1, 0)
+        xi("v", 1, 1, 1)
+        xi("s", 1, 0, 1)
+        xq(0, 0, 1)
+        xi("v", 1, 0, 2)
+        m1(1, 0, 0)
         bl(0, 0)
-        bl(0, 1)
-        c_phi("s", 3, 1)
+        t_phi(3)
+        m1(1, 0, 1)
         xq(1, 1, 1)
+        load_phi(1)
+        bl(0, 1)
+        c_phi("s", 0, 0)
+        c_phi("s", 0, 1)
+        m1(0, 1, 0)
+        c_phi("s", 3, 1)
+        xq(1, 0, 1)
+        t_phi(2)
+        q_phi(0)
+        t_phi(1)
         i_cg(CH[0])
-        q_phi(1)
         c_phi("s", 3, 0)
+        sc(1, 0)
+        c_phi("s", 2, 0)
+        m1(0, 1, 1)
+        xq(1, 0, 2)
         c_phi("s", 2, 1)
+        c_phi("s", 1, 0)
         q_cg(CH[0])
-        c_phi("v", 2, 0)
-        m1(0, 2, 0)
-        q_phi(3)
         m2(0, 0)
-        q_phi(2)
-        m1(1, 1, 1)
-        bl(1, 1)
         m1(1, 1, 0)
-        bl(1, 0)
-        sc(2, 0)
+        q_phi(2)
         m2(2, 0)
+        q_phi(3)
+        xq(1, 1, 2)
+        c_phi("s", 1, 1)
+        q_phi(1)
+        bl(1, 0)
+        sc(1, 1)
         A(0, 0, "ss")
-        B(0, 0)
-        i_cg(CH[1])
-        A(2, 0, "ss")
-        B(2, 0)
-        m1(1, 2, 0)
-        q_cg(CH[1])
-        bl(2, 0)
+        m1(1, 1, 1)
         m2(3, 0)
-        m2(1, 0)
+        A(2, 0, "ss")
         A(3, 0, "ss")
-        m1(1, 2, 1)
-        m1(0, 2, 1)
-        m2(3, 1)
-        A(1, 0, "ss")
+        bl(1, 1)
+        B(0, 0)
+        m1(0, 2, 0)
+        sc(2, 0)
+        i_cg(CH[1])
+        m2(1, 0)
         Q(0, 0)
-        sc(2, 1)
-        B(1, 0)
-        Q(2, 0)
-        Q(1, 0)
-        bl(2, 1)
-        A(3, 1, "ss")
-        B(3, 0)
-        m2(1, 1)
-        A(1, 1, "ss")
-        m2(2, 1)
-        i_cg(CH[2])
-        Q(3, 0)
-        A(2, 1, "ss")
+        q_cg(CH[1])
+        A(1, 0, "sv")
+        m1(1, 2, 0)
+        m1(1, 2, 1)
         m2(0, 1)
-        q_cg(CH[2])
-        m2(2, 2)
+        bl(2, 0)
         A(0, 1, "ss")
-        m2(3, 2)
-        B(3, 1)
-        B(2, 1)
-        m2(1, 2)
+        B(3, 0)
+        m1(0, 2, 1)
+        sc(2, 1)
+        B(2, 0)
+        m2(1, 1)
+        Q(3, 0)
+        Q(2, 0)
+        bl(2, 1)
+        B(1, 0)
+        m2(2, 1)
+        m2(3, 1)
+        A(2, 1, "ss")
+        A(1, 1, "ss")
+        i_cg(CH[2])
+        Q(1, 0)
+        q_cg(CH[2])
         B(1, 1)
-        Q(3, 1)
-        Q(2, 1)
-        A(2, 2, "ss")
-        B(0, 1)
+        B(2, 1)
+        A(3, 1, "ss")
         Q(1, 1)
-        A(3, 2, "ss")
-        B(2, 2)
         m2(0, 2)
-        A(1, 2, "vv")
-        Q(0, 1)
-        store_s(0, 4, 0, 512)
-        B(1, 2)
-        B(3, 2)
-        Q(1, 2)
         A(0, 2, "ss")
-        Q(3, 2)
+        m2(3, 2)
+        B(0, 1)
+        Q(2, 1)
+        Q(0, 1)
+        B(3, 1)
+        A(3, 2, "ss")
+        B(3, 2)
+        Q(3, 1)
+        m2(1, 2)
+        A(1, 2, "ss")
+        B(1, 2)
+        store_s(0, 4, 0, 512)
+        m2(2, 2)
         B(0, 2)
+        Q(1, 2)
+        A(2, 2, "ss")
+        B(2, 2)
+        Q(3, 2)
         Q(2, 2)
         Q(0, 2)
         store_s(0, 4, 512, 768)

@@ -54,10 +54,10 @@ def tile_coupledbasisspectralposetransfer_x1_kernel(
                 in_=psi_in[b][512 * q : 512 * q + 512, :].rearrange("(p j) c -> p j c", j=4),
             )
 
-        def load_x(b, q):
+        def load_x(b, q, a, z):
             nc.sync.dma_start(
-                out=x_raw[b, q][:],
-                in_=x_in[b][512 * q : 512 * q + 512, :].rearrange("(p j) c -> p j c", j=4),
+                out=x_raw[b, q][:, :, a:z],
+                in_=x_in[b][512 * q : 512 * q + 512, a:z].rearrange("(p j) c -> p j c", j=4),
             )
 
         def load_phi(gg):
@@ -129,9 +129,12 @@ def tile_coupledbasisspectralposetransfer_x1_kernel(
                 src.rearrange("p t (c i) -> p c t i", i=4),
             )
 
-        def i_psi(eng, b, q, t0, t1):
-            src = psi_raw[b, q][:].rearrange("p j (m t) -> p t m j", t=4)
-            copy(eng, psi_grp[b, q][:, t0:t1], src[:, t0:t1])
+        def i_psi(eng, b, q, m0, m1):
+            copy(
+                eng,
+                psi_grp[b, q][:, :, m0:m1, :].rearrange("p t m j -> p m j t"),
+                psi_raw[b, q][:].rearrange("p j (m t) -> p m j t", t=4)[:, m0:m1],
+            )
 
         def q_psi(b, q):
             quant(psi_c[b, q][:], psi_s[b, q][:], psi_grp[b, q][:].rearrange("p t m j -> p (t m j)"))
@@ -186,8 +189,8 @@ def tile_coupledbasisspectralposetransfer_x1_kernel(
                     in1=part1[:, t, ch[0] : ch[1]], op0=ALU.mult, op1=ALU.add,
                 )
 
-        def i_cg(ch):
-            interleave("v", cg_grp[ch][:], cg_flat[ch][:])
+        def i_cg(eng, ch):
+            interleave(eng, cg_grp[ch][:], cg_flat[ch][:])
 
         def q_cg(ch):
             quant(cg_c[ch][:], cg_s[ch][:], cg_grp[ch][:].rearrange("p n j -> p (n j)"))
@@ -240,12 +243,12 @@ def tile_coupledbasisspectralposetransfer_x1_kernel(
                 in_=out_f[gg, ch][:, :, a:z],
             )
 
-        def round_out(gg, ch, a, z):
+        def round_out(eng, gg, ch, a, z):
             if a == 0:
                 w = ch[1] - ch[0]
                 out_b[gg, ch] = work.tile([P, w, 4], BF16, name="out_b", bufs=4, align_bytes=64)
                 out_c[gg, ch] = work.tile([P, w], U32, name="out_c", bufs=6, align_bytes=64)
-            interleave("v", out_b[gg, ch][:, a:z, :], out_f[gg, ch][:, :, a:z])
+            interleave(eng, out_b[gg, ch][:, a:z, :], out_f[gg, ch][:, :, a:z])
 
         def q_out(gg, ch, a, z):
             quant(
@@ -257,9 +260,9 @@ def tile_coupledbasisspectralposetransfer_x1_kernel(
                 in_=out_c[gg, ch][:, a:z].bitcast(I32),
             )
 
-        def store_s(g0, g1, a, z):
+        def store_s(queue, g0, g1, a, z):
             for quad in range(4):
-                nc.sync.dma_start(
+                queue.dma_start(
                     out=out_2[g0:g1, 4 * quad : 4 * quad + 4, a:z].bitcast(I32).rearrange("g q n -> q g n"),
                     in_=out_s[32 * quad : 32 * quad + 4, g0:g1, a:z].bitcast(I32),
                 )
@@ -288,153 +291,157 @@ def tile_coupledbasisspectralposetransfer_x1_kernel(
             empty(gg, CH[c], engines)
             store_f(gg, CH[c], 0, 256)
 
-        def B(gg, c):
-            round_out(gg, CH[c], 0, 256)
+        def B(eng, gg, c):
+            round_out(eng, gg, CH[c], 0, 256)
 
         def Q(gg, c):
             q_out(gg, CH[c], 0, 256)
 
         load_psi(0, 0)
-        i_psi("v", 0, 0, 2, 4)
-        i_psi("s", 0, 0, 0, 2)
-        load_psi(0, 1)
-        i_psi("v", 0, 1, 0, 2)
-        i_psi("s", 0, 1, 2, 4)
-        q_psi(0, 1)
-        load_x(0, 1)
-        xi("v", 0, 1, 2)
-        load_x(0, 0)
-        load_psi(1, 0)
-        q_psi(0, 0)
-        xq(0, 1, 2)
-        xi("s", 0, 1, 1)
-        load_x(1, 1)
-        xi("v", 0, 0, 2)
-        xi("s", 0, 1, 0)
-        i_psi("v", 1, 0, 2, 4)
-        load_psi(1, 1)
-        i_psi("v", 1, 0, 0, 2)
-        xq(0, 1, 0)
-        xi("s", 0, 0, 1)
-        load_x(1, 0)
-        xq(0, 1, 1)
-        q_psi(1, 0)
-        load_phi(0)
+        load_x(0, 0, 0, 256)
+        i_psi("v", 0, 0, 0, 64)
+        i_psi("v", 0, 0, 64, 128)
         xi("s", 0, 0, 0)
-        xq(0, 0, 2)
+        load_psi(0, 1)
+        i_psi("v", 0, 1, 64, 128)
+        load_x(0, 1, 256, 768)
         xq(0, 0, 0)
-        i_psi("v", 1, 1, 2, 4)
-        xi("s", 1, 1, 0)
-        xi("v", 1, 1, 2)
-        load_phi(3)
-        xi("v", 1, 0, 0)
+        q_psi(0, 0)
+        load_x(0, 1, 0, 256)
+        i_psi("s", 0, 1, 0, 64)
+        q_psi(0, 1)
+        xi("v", 0, 1, 0)
+        xi("s", 0, 1, 2)
+        load_psi(1, 1)
+        xi("v", 0, 1, 1)
+        xq(0, 1, 0)
+        load_x(0, 0, 256, 768)
         m1(0, 0, 1)
-        xq(1, 1, 0)
-        load_phi(2)
-        i_psi("s", 1, 1, 0, 2)
-        sc(0, 1)
-        xq(1, 0, 0)
+        i_psi("s", 1, 1, 64, 128)
+        xq(0, 1, 1)
+        load_psi(1, 0)
+        load_x(1, 0, 0, 256)
+        xq(0, 1, 2)
+        i_psi("s", 1, 1, 0, 64)
+        xi("v", 0, 0, 2)
+        xi("v", 0, 0, 1)
+        xq(0, 0, 2)
+        i_psi("s", 1, 0, 0, 64)
+        i_psi("s", 1, 0, 64, 128)
         m1(0, 0, 0)
-        q_psi(1, 1)
-        t_phi(0)
-        sc(0, 0)
-        xi("v", 1, 1, 1)
-        xi("s", 1, 0, 1)
+        load_x(1, 1, 0, 256)
         xq(0, 0, 1)
-        xi("v", 1, 0, 2)
-        m1(1, 0, 0)
-        bl(0, 0)
-        t_phi(3)
-        m1(1, 0, 1)
-        xq(1, 1, 1)
-        load_phi(1)
-        bl(0, 1)
-        c_phi("s", 0, 0)
-        c_phi("s", 0, 1)
+        q_psi(1, 1)
+        load_phi(0)
+        xi("v", 1, 1, 0)
         m1(0, 1, 0)
-        c_phi("s", 3, 1)
-        xq(1, 0, 1)
-        t_phi(2)
-        q_phi(0)
-        t_phi(1)
-        i_cg(CH[0])
-        c_phi("s", 3, 0)
+        m1(0, 2, 0)
+        sc(0, 1)
+        sc(2, 0)
+        load_x(1, 0, 256, 768)
+        t_phi(0)
+        xi("v", 1, 0, 0)
+        m1(0, 2, 1)
+        xq(1, 1, 0)
+        xq(1, 0, 0)
+        q_psi(1, 0)
+        m1(1, 0, 0)
         sc(1, 0)
-        c_phi("s", 2, 0)
+        sc(0, 0)
+        load_phi(1)
+        xi("v", 1, 0, 2)
+        xi("v", 1, 0, 1)
+        sc(2, 1)
+        bl(0, 0)
+        load_x(1, 1, 256, 768)
+        xi("v", 1, 1, 1)
+        c_phi("s", 0, 1)
+        m1(1, 0, 1)
+        t_phi(1)
+        bl(0, 1)
+        load_phi(2)
+        xq(1, 0, 1)
+        load_phi(3)
+        i_cg("v", CH[0])
+        xq(1, 1, 1)
         m1(0, 1, 1)
-        xq(1, 0, 2)
-        c_phi("s", 2, 1)
+        c_phi("s", 0, 0)
+        t_phi(2)
+        xi("s", 1, 1, 2)
+        m1(1, 1, 0)
+        q_phi(0)
+        c_phi("s", 1, 1)
         c_phi("s", 1, 0)
         q_cg(CH[0])
-        m2(0, 0)
-        m1(1, 1, 0)
-        q_phi(2)
-        m2(2, 0)
-        q_phi(3)
-        xq(1, 1, 2)
-        c_phi("s", 1, 1)
-        q_phi(1)
+        m1(1, 1, 1)
         bl(1, 0)
         sc(1, 1)
-        A(0, 0, "ss")
-        m1(1, 1, 1)
-        m2(3, 0)
-        A(2, 0, "ss")
-        A(3, 0, "ss")
-        bl(1, 1)
-        B(0, 0)
-        m1(0, 2, 0)
-        sc(2, 0)
-        i_cg(CH[1])
+        q_phi(1)
+        m2(0, 0)
         m2(1, 0)
-        Q(0, 0)
+        c_phi("v", 2, 1)
+        c_phi("s", 2, 0)
+        bl(1, 1)
+        t_phi(3)
+        q_phi(2)
+        A(0, 0, "ss")
+        A(1, 0, "ss")
+        i_cg("v", CH[1])
+        xq(1, 0, 2)
+        c_phi("s", 3, 0)
+        m2(2, 0)
+        c_phi("s", 3, 1)
         q_cg(CH[1])
-        A(1, 0, "sv")
-        m1(1, 2, 0)
-        m1(1, 2, 1)
-        m2(0, 1)
-        bl(2, 0)
-        A(0, 1, "ss")
-        B(3, 0)
-        m1(0, 2, 1)
-        sc(2, 1)
-        B(2, 0)
         m2(1, 1)
-        Q(3, 0)
-        Q(2, 0)
-        bl(2, 1)
-        B(1, 0)
-        m2(2, 1)
-        m2(3, 1)
-        A(2, 1, "ss")
+        A(2, 0, "sv")
+        xq(1, 1, 2)
         A(1, 1, "ss")
-        i_cg(CH[2])
+        m2(0, 1)
+        m2(2, 1)
+        A(0, 1, "ss")
+        m1(1, 2, 1)
+        q_phi(3)
+        B("v", 0, 0)
+        m2(3, 0)
+        B("v", 1, 0)
+        bl(2, 1)
+        A(2, 1, "ss")
+        Q(0, 0)
+        B("s", 0, 1)
+        m1(1, 2, 0)
+        bl(2, 0)
+        m2(3, 1)
         Q(1, 0)
-        q_cg(CH[2])
-        B(1, 1)
-        B(2, 1)
-        A(3, 1, "ss")
-        Q(1, 1)
-        m2(0, 2)
-        A(0, 2, "ss")
-        m2(3, 2)
-        B(0, 1)
-        Q(2, 1)
+        B("v", 2, 1)
         Q(0, 1)
-        B(3, 1)
-        A(3, 2, "ss")
-        B(3, 2)
-        Q(3, 1)
+        A(3, 0, "ss")
+        i_cg("v", CH[2])
+        B("v", 2, 0)
+        q_cg(CH[2])
+        A(3, 1, "ss")
         m2(1, 2)
+        Q(2, 1)
+        B("v", 1, 1)
+        B("s", 3, 0)
+        Q(2, 0)
+        m2(0, 2)
+        Q(1, 1)
+        Q(3, 0)
         A(1, 2, "ss")
-        B(1, 2)
-        store_s(0, 4, 0, 512)
+        B("v", 3, 1)
+        Q(3, 1)
         m2(2, 2)
-        B(0, 2)
-        Q(1, 2)
+        A(0, 2, "ss")
+        store_s(nc.sync, 0, 4, 0, 512)
         A(2, 2, "ss")
-        B(2, 2)
-        Q(3, 2)
-        Q(2, 2)
+        m2(3, 2)
+        B("v", 0, 2)
         Q(0, 2)
-        store_s(0, 4, 512, 768)
+        A(3, 2, "ss")
+        B("v", 1, 2)
+        B("v", 2, 2)
+        Q(1, 2)
+        Q(2, 2)
+        B("s", 3, 2)
+        Q(3, 2)
+        store_s(nc.scalar, 0, 4, 512, 768)

@@ -15,7 +15,7 @@ ACT = mybir.ActivationFunctionType
 V, K, N, R = 1024, 512, 768, 2048
 P = 128
 G = R // 512
-CH = ((0, 256), (256, 512), (512, 768))
+CH = ((0, 512), (512, 768))
 FLOPS = 2 * (2 * V * K * N + R * K * N)
 
 
@@ -54,10 +54,10 @@ def tile_coupledbasisspectralposetransfer_x1_kernel(
                 in_=psi_in[b][512 * q : 512 * q + 512, :].rearrange("(p j) c -> p j c", j=4),
             )
 
-        def load_x(b, q, a, z):
+        def load_x(b, q):
             nc.sync.dma_start(
-                out=x_raw[b, q][:, :, a:z],
-                in_=x_in[b][512 * q : 512 * q + 512, a:z].rearrange("(p j) c -> p j c", j=4),
+                out=x_raw[b, q][:],
+                in_=x_in[b][512 * q : 512 * q + 512, :].rearrange("(p j) c -> p j c", j=4),
             )
 
         def load_phi(gg):
@@ -93,7 +93,7 @@ def tile_coupledbasisspectralposetransfer_x1_kernel(
             for q in range(2):
                 tag = "%d%d" % (b, q)
                 psi_grp[b, q] = kept([P, 4, P, 4], BF16, "psi_grp_" + tag)
-                x_grp[b, q] = kept([P, N, 4], BF16, "x_grp_" + tag)
+                x_grp[b, q] = keep.tile([P, N, 4], BF16, name="x_grp_" + tag, tag="columns", bufs=4, align_bytes=64)
                 psi_c[b, q] = kept([P, K], U32, "psi_c_" + tag)
                 psi_s[b, q] = kept([P, K], U8, "psi_s_" + tag)
                 x_c[b, q] = kept([P, N], U32, "x_c_" + tag)
@@ -189,11 +189,11 @@ def tile_coupledbasisspectralposetransfer_x1_kernel(
                     in1=part1[:, t, ch[0] : ch[1]], op0=ALU.mult, op1=ALU.add,
                 )
 
-        def i_cg(eng, ch):
-            interleave(eng, cg_grp[ch][:], cg_flat[ch][:])
+        def i_cg(eng, c, a, z):
+            interleave(eng, cg_grp[CH[c]][:, a:z, :], cg_flat[CH[c]][:, :, a:z])
 
-        def q_cg(ch):
-            quant(cg_c[ch][:], cg_s[ch][:], cg_grp[ch][:].rearrange("p n j -> p (n j)"))
+        def q_cg(c):
+            quant(cg_c[CH[c]][:], cg_s[CH[c]][:], cg_grp[CH[c]][:].rearrange("p n j -> p (n j)"))
 
         def t_phi(gg):
             words = phi_raw[gg][:].rearrange("p t k -> p (t k)").bitcast(F32)
@@ -216,232 +216,247 @@ def tile_coupledbasisspectralposetransfer_x1_kernel(
         def q_phi(gg):
             quant(phi_c[gg][:], phi_s[gg][:], phi_grp[gg][:].rearrange("p t m j -> p (t m j)"))
 
-        out_f, out_b, out_c = {}, {}, {}
-
-        def mm2(gg, ch):
-            w = ch[1] - ch[0]
-            per = 512 // w
-            for i in range(4 // per):
-                acc = psum.tile([P, per, w], F32, name="acc2", tag="bank")
-                bank["out", gg, ch, i] = acc
-                for k in range(per):
-                    mm(
-                        acc[:, k, :], phi_c[gg], phi_s[gg], P * (per * i + k),
-                        cg_c[ch], cg_s[ch], 0, w, True, True,
-                    )
-
-        def empty(gg, ch, engines):
-            w = ch[1] - ch[0]
-            per = 512 // w
-            out_f[gg, ch] = work.tile([P, 4, w], F32, name="out_f", bufs=6, align_bytes=64)
-            for i in range(4 // per):
-                copy(engines[i], out_f[gg, ch][:, per * i : per * i + per, :], bank["out", gg, ch, i][:])
-
-        def store_f(gg, ch, a, z):
-            nc.sync.dma_start(
-                out=out_0[512 * gg : 512 * gg + 512, ch[0] + a : ch[0] + z].rearrange("(p t) n -> p t n", t=4),
-                in_=out_f[gg, ch][:, :, a:z],
-            )
-
-        def round_out(eng, gg, ch, a, z):
-            if a == 0:
-                w = ch[1] - ch[0]
-                out_b[gg, ch] = work.tile([P, w, 4], BF16, name="out_b", bufs=4, align_bytes=64)
-                out_c[gg, ch] = work.tile([P, w], U32, name="out_c", bufs=6, align_bytes=64)
-            interleave(eng, out_b[gg, ch][:, a:z, :], out_f[gg, ch][:, :, a:z])
-
-        def q_out(gg, ch, a, z):
-            quant(
-                out_c[gg, ch][:, a:z], out_s[:, gg, ch[0] + a : ch[0] + z],
-                out_b[gg, ch][:, a:z, :].rearrange("p n j -> p (n j)"),
-            )
-            nc.sync.dma_start(
-                out=out_1[gg, :, ch[0] + a : ch[0] + z, :].rearrange("p n t -> p (n t)").bitcast(I32),
-                in_=out_c[gg, ch][:, a:z].bitcast(I32),
-            )
-
-        def store_s(queue, g0, g1, a, z):
-            for quad in range(4):
-                queue.dma_start(
-                    out=out_2[g0:g1, 4 * quad : 4 * quad + 4, a:z].bitcast(I32).rearrange("g q n -> q g n"),
-                    in_=out_s[32 * quad : 32 * quad + 4, g0:g1, a:z].bitcast(I32),
-                )
-
-        T01, T23 = (0, 1), (2, 3)
-
         def xi(eng, b, q, c):
             i_x(eng, b, q, 256 * c, 256 * c + 256)
 
         def xq(b, q, c):
-            q_x(b, q, 256 * c, 256 * c + 256)
+            q_x(b, q, CH[c][0], CH[c][1])
+
+        SLOTS = (((0,), (1,), (2,), (3,)), ((0, 1), (2, 3)))
 
         def m1(b, c, h):
-            mm1(b, CH[c], (T01, T23)[h])
+            mm1(b, CH[c], SLOTS[c][h])
 
         def sc(c, h):
-            scale1(CH[c], (T01, T23)[h])
+            scale1(CH[c], SLOTS[c][h])
 
         def bl(c, h):
-            blend(CH[c], (T01, T23)[h])
+            blend(CH[c], SLOTS[c][h])
 
-        def m2(gg, c):
-            mm2(gg, CH[c])
+        out_f, out_b, out_c = {}, {}, {}
 
-        def A(gg, c, engines):
-            empty(gg, CH[c], engines)
-            store_f(gg, CH[c], 0, 256)
+        def m2(gg, c, h):
+            ts = SLOTS[c][h]
+            w = CH[c][1] - CH[c][0]
+            acc = psum.tile([P, len(ts), w], F32, name="acc2", tag="bank")
+            bank["out", gg, c, h] = acc
+            for i in range(len(ts)):
+                mm(
+                    acc[:, i, :], phi_c[gg], phi_s[gg], P * ts[i],
+                    cg_c[CH[c]], cg_s[CH[c]], 0, w, True, True,
+                )
+
+        def A(eng, gg, c, h):
+            if gg not in out_f:
+                out_f[gg] = work.tile([P, 4, N], F32, name="out_f", bufs=3, align_bytes=64)
+            ts = SLOTS[c][h]
+            copy(
+                eng,
+                out_f[gg][:, ts[0] : ts[0] + len(ts), CH[c][0] : CH[c][1]],
+                bank["out", gg, c, h][:],
+            )
+
+        def store_f(gg, t0, t1):
+            nc.sync.dma_start(
+                out=out_0[512 * gg : 512 * gg + 512, :].rearrange("(p t) n -> p t n", t=4)[:, t0:t1, :],
+                in_=out_f[gg][:, t0:t1, :],
+            )
 
         def B(eng, gg, c):
-            round_out(eng, gg, CH[c], 0, 256)
+            if gg not in out_b:
+                out_b[gg] = keep.tile([P, N, 4], BF16, name="out_b", tag="columns", bufs=4, align_bytes=64)
+                out_c[gg] = work.tile([P, N], U32, name="out_c", bufs=3, align_bytes=64)
+            a = 256 * c
+            interleave(eng, out_b[gg][:, a : a + 256, :], out_f[gg][:, :, a : a + 256])
 
         def Q(gg, c):
-            q_out(gg, CH[c], 0, 256)
+            a, z = CH[c]
+            quant(
+                out_c[gg][:, a:z], out_s[:, gg, a:z],
+                out_b[gg][:, a:z, :].rearrange("p n j -> p (n j)"),
+            )
 
-        load_psi(0, 0)
-        load_x(0, 0, 0, 256)
-        i_psi("v", 0, 0, 0, 64)
-        i_psi("v", 0, 0, 64, 128)
-        xi("s", 0, 0, 0)
+        def store_c(gg):
+            nc.sync.dma_start(
+                out=out_1[gg].rearrange("p n t -> p (n t)").bitcast(I32),
+                in_=out_c[gg][:].bitcast(I32),
+            )
+
+        def store_s(queue, g0, g1):
+            for quad in range(4):
+                queue.dma_start(
+                    out=out_2[g0:g1, 4 * quad : 4 * quad + 4, :].bitcast(I32).rearrange("g q n -> q g n"),
+                    in_=out_s[32 * quad : 32 * quad + 4, g0:g1, :].bitcast(I32),
+                )
+
         load_psi(0, 1)
-        i_psi("v", 0, 1, 64, 128)
-        load_x(0, 1, 256, 768)
-        xq(0, 0, 0)
-        q_psi(0, 0)
-        load_x(0, 1, 0, 256)
         i_psi("s", 0, 1, 0, 64)
-        q_psi(0, 1)
-        xi("v", 0, 1, 0)
-        xi("s", 0, 1, 2)
-        load_psi(1, 1)
-        xi("v", 0, 1, 1)
-        xq(0, 1, 0)
-        load_x(0, 0, 256, 768)
-        m1(0, 0, 1)
-        i_psi("s", 1, 1, 64, 128)
-        xq(0, 1, 1)
+        i_psi("v", 0, 1, 64, 128)
+        load_psi(0, 0)
+        i_psi("v", 0, 0, 0, 64)
+        load_x(0, 1)
+        load_x(0, 0)
         load_psi(1, 0)
-        load_x(1, 0, 0, 256)
-        xq(0, 1, 2)
-        i_psi("s", 1, 1, 0, 64)
-        xi("v", 0, 0, 2)
-        xi("v", 0, 0, 1)
-        xq(0, 0, 2)
-        i_psi("s", 1, 0, 0, 64)
+        q_psi(0, 1)
+        i_psi("s", 0, 0, 64, 128)
+        xi("s", 0, 1, 1)
+        xi("v", 0, 1, 2)
+        load_x(1, 0)
+        load_x(1, 1)
+        xi("v", 0, 1, 0)
+        xi("s", 0, 0, 2)
         i_psi("s", 1, 0, 64, 128)
-        m1(0, 0, 0)
-        load_x(1, 1, 0, 256)
+        xq(0, 1, 1)
+        xq(0, 1, 0)
+        xi("v", 0, 0, 1)
+        xi("v", 0, 0, 0)
+        xi("s", 1, 0, 1)
         xq(0, 0, 1)
-        q_psi(1, 1)
-        load_phi(0)
-        xi("v", 1, 1, 0)
-        m1(0, 1, 0)
-        m1(0, 2, 0)
-        sc(0, 1)
-        sc(2, 0)
-        load_x(1, 0, 256, 768)
-        t_phi(0)
-        xi("v", 1, 0, 0)
-        m1(0, 2, 1)
-        xq(1, 1, 0)
-        xq(1, 0, 0)
-        q_psi(1, 0)
-        m1(1, 0, 0)
-        sc(1, 0)
-        sc(0, 0)
-        load_phi(1)
+        q_psi(0, 0)
+        xq(0, 0, 0)
+        xi("s", 1, 0, 0)
+        m1(0, 0, 0)
         xi("v", 1, 0, 2)
-        xi("v", 1, 0, 1)
-        sc(2, 1)
-        bl(0, 0)
-        load_x(1, 1, 256, 768)
+        i_psi("v", 1, 0, 0, 64)
         xi("v", 1, 1, 1)
-        c_phi("s", 0, 1)
-        m1(1, 0, 1)
-        t_phi(1)
-        bl(0, 1)
-        load_phi(2)
-        xq(1, 0, 1)
-        load_phi(3)
-        i_cg("v", CH[0])
-        xq(1, 1, 1)
+        m1(0, 0, 2)
         m1(0, 1, 1)
-        c_phi("s", 0, 0)
-        t_phi(2)
-        xi("s", 1, 1, 2)
-        m1(1, 1, 0)
-        q_phi(0)
-        c_phi("s", 1, 1)
-        c_phi("s", 1, 0)
-        q_cg(CH[0])
-        m1(1, 1, 1)
-        bl(1, 0)
+        xi("s", 1, 1, 0)
+        load_psi(1, 1)
+        i_psi("s", 1, 1, 0, 64)
+        sc(0, 2)
+        xq(1, 0, 1)
+        load_phi(0)
+        xq(1, 0, 0)
+        sc(0, 0)
+        m1(0, 0, 3)
+        i_psi("v", 1, 1, 64, 128)
         sc(1, 1)
-        q_phi(1)
-        m2(0, 0)
-        m2(1, 0)
-        c_phi("v", 2, 1)
-        c_phi("s", 2, 0)
+        t_phi(0)
+        q_psi(1, 0)
+        m1(0, 0, 1)
+        xq(1, 1, 0)
+        q_psi(1, 1)
+        m1(1, 0, 2)
+        load_phi(3)
+        xi("v", 1, 1, 2)
+        m1(1, 0, 0)
+        bl(0, 2)
+        c_phi("s", 0, 0)
+        sc(0, 3)
+        m1(1, 0, 3)
+        bl(0, 0)
+        sc(0, 1)
+        m1(1, 0, 1)
+        xq(1, 1, 1)
+        c_phi("s", 0, 1)
+        m1(0, 1, 0)
+        bl(0, 3)
+        bl(0, 1)
+        load_phi(1)
+        m1(1, 1, 1)
         bl(1, 1)
+        sc(1, 0)
+        m1(1, 1, 0)
         t_phi(3)
-        q_phi(2)
-        A(0, 0, "ss")
-        A(1, 0, "ss")
-        i_cg("v", CH[1])
-        xq(1, 0, 2)
+        bl(1, 0)
+        q_phi(0)
+        i_cg("s", 0, 0, 256)
+        t_phi(1)
+        i_cg("v", 1, 0, 256)
+        i_cg("s", 0, 256, 512)
         c_phi("s", 3, 0)
-        m2(2, 0)
+        q_cg(1)
+        q_cg(0)
         c_phi("s", 3, 1)
-        q_cg(CH[1])
-        m2(1, 1)
-        A(2, 0, "sv")
-        xq(1, 1, 2)
-        A(1, 1, "ss")
-        m2(0, 1)
-        m2(2, 1)
-        A(0, 1, "ss")
-        m1(1, 2, 1)
+        c_phi("v", 1, 1)
+        m2(0, 1, 1)
         q_phi(3)
-        B("v", 0, 0)
-        m2(3, 0)
-        B("v", 1, 0)
-        bl(2, 1)
-        A(2, 1, "ss")
-        Q(0, 0)
-        B("s", 0, 1)
-        m1(1, 2, 0)
-        bl(2, 0)
-        m2(3, 1)
-        Q(1, 0)
-        B("v", 2, 1)
-        Q(0, 1)
-        A(3, 0, "ss")
-        i_cg("v", CH[2])
-        B("v", 2, 0)
-        q_cg(CH[2])
-        A(3, 1, "ss")
-        m2(1, 2)
-        Q(2, 1)
-        B("v", 1, 1)
-        B("s", 3, 0)
-        Q(2, 0)
-        m2(0, 2)
-        Q(1, 1)
-        Q(3, 0)
-        A(1, 2, "ss")
+        m2(0, 0, 2)
+        A("v", 0, 0, 2)
+        c_phi("s", 1, 0)
+        m2(0, 0, 3)
+        q_phi(1)
+        A("s", 0, 1, 1)
+        m2(3, 0, 3)
+        m2(3, 0, 2)
+        m2(3, 1, 1)
+        A("s", 0, 0, 3)
+        load_phi(2)
+        A("s", 3, 0, 2)
+        store_f(0, 2, 4)
+        m2(3, 0, 0)
+        A("s", 3, 0, 0)
+        A("v", 3, 0, 3)
+        m2(3, 0, 1)
+        m2(1, 0, 2)
+        m2(3, 1, 0)
+        A("s", 1, 0, 2)
+        m2(0, 0, 0)
+        A("s", 0, 0, 0)
+        A("v", 3, 1, 1)
+        A("v", 3, 0, 1)
+        A("v", 3, 1, 0)
+        m2(1, 1, 1)
+        A("s", 1, 1, 1)
+        store_f(3, 2, 4)
+        m2(1, 0, 3)
         B("v", 3, 1)
-        Q(3, 1)
-        m2(2, 2)
-        A(0, 2, "ss")
-        store_s(nc.sync, 0, 4, 0, 512)
-        A(2, 2, "ss")
-        m2(3, 2)
+        m2(0, 1, 0)
+        B("v", 3, 2)
+        A("v", 0, 1, 0)
+        t_phi(2)
+        m2(1, 0, 1)
+        A("s", 1, 0, 3)
+        store_f(3, 0, 2)
+        store_f(1, 2, 4)
+        B("v", 3, 0)
+        m2(0, 0, 1)
+        A("v", 0, 0, 1)
+        c_phi("s", 2, 0)
+        c_phi("s", 2, 1)
+        A("s", 1, 0, 1)
+        m2(1, 1, 0)
+        m2(1, 0, 0)
+        A("s", 1, 1, 0)
+        q_phi(2)
+        m2(2, 1, 1)
+        A("s", 1, 0, 0)
+        B("v", 0, 1)
+        store_f(0, 0, 2)
+        B("s", 1, 2)
+        m2(2, 0, 1)
         B("v", 0, 2)
-        Q(0, 2)
-        A(3, 2, "ss")
-        B("v", 1, 2)
+        Q(3, 1)
+        m2(2, 1, 0)
+        A("s", 2, 1, 1)
+        A("s", 2, 0, 1)
+        m2(2, 0, 0)
+        A("s", 2, 0, 0)
+        B("v", 1, 0)
+        m2(2, 0, 3)
+        B("s", 0, 0)
+        m2(2, 0, 2)
+        Q(3, 0)
+        store_f(1, 0, 2)
+        A("v", 2, 0, 3)
+        A("v", 2, 0, 2)
+        Q(1, 1)
+        B("v", 1, 1)
+        B("v", 2, 1)
+        A("s", 2, 1, 0)
+        Q(1, 0)
+        Q(0, 1)
+        store_c(3)
+        Q(0, 0)
+        store_f(2, 2, 4)
+        store_s(nc.scalar, 3, 4)
+        store_f(2, 0, 2)
+        store_c(0)
+        B("s", 2, 0)
         B("v", 2, 2)
-        Q(1, 2)
-        Q(2, 2)
-        B("s", 3, 2)
-        Q(3, 2)
-        store_s(nc.scalar, 0, 4, 512, 768)
+        Q(2, 0)
+        store_c(1)
+        Q(2, 1)
+        store_s(nc.sync, 0, 3)
+        store_c(2)

from contextlib import ExitStack

import concourse.mybir as mybir
from concourse.masks import make_identity

F32 = mybir.dt.float32
BF16 = mybir.dt.bfloat16
I32 = mybir.dt.int32
U32 = mybir.dt.uint32
U8 = mybir.dt.uint8
FP8X4 = mybir.dt.float8_e4m3fn_x4
ALU = mybir.AluOpType
ACT = mybir.ActivationFunctionType

V, K, N, R = 1024, 512, 768, 2048
P = 128
G = R // 512
CH = ((0, 512), (512, 768))
FLOPS = 2 * (2 * V * K * N + R * K * N)


def tile_coupledbasisspectralposetransfer_x1_kernel(
    tc, psi1, x1, psi2, x2, lam, g, phi3, out_0, out_1, out_2
):
    nc = tc.nc
    psi_in = (psi1, psi2)
    x_in = (x1, x2)

    with ExitStack() as ctx:
        keep = ctx.enter_context(tc.tile_pool(name="keep", bufs=1))
        work = ctx.enter_context(tc.tile_pool(name="work", bufs=2))
        psum = ctx.enter_context(tc.psum_pool(name="psum", bufs=8))
        ctx.enter_context(tc.manual_schedule())

        def kept(shape, dtype, name):
            return keep.tile(shape, dtype, name=name, align_bytes=64)

        lam_t = kept([P, 4], BF16, "lam_t")
        g_t = kept([P, 4], BF16, "g_t")
        nc.scalar.dma_start(out=lam_t[:], in_=lam.rearrange("(p t) -> p t", t=4))
        nc.scalar.dma_start(out=g_t[:], in_=g.rearrange("(p t) -> p t", t=4))

        psi_raw, x_raw, phi_raw = {}, {}, {}
        for b in range(2):
            for q in range(2):
                psi_raw[b, q] = kept([P, 4, K], BF16, "psi_raw_%d%d" % (b, q))
                x_raw[b, q] = kept([P, 4, N], BF16, "x_raw_%d%d" % (b, q))
        for gg in range(G):
            phi_raw[gg] = kept([P, 4, K], BF16, "phi_raw_%d" % gg)

        def load_psi(b, q):
            nc.sync.dma_start(
                out=psi_raw[b, q][:],
                in_=psi_in[b][512 * q : 512 * q + 512, :].rearrange("(p j) c -> p j c", j=4),
            )

        def load_x(b, q):
            nc.sync.dma_start(
                out=x_raw[b, q][:],
                in_=x_in[b][512 * q : 512 * q + 512, :].rearrange("(p j) c -> p j c", j=4),
            )

        def load_phi(gg):
            nc.sync.dma_start(
                out=phi_raw[gg][:],
                in_=phi3[512 * gg : 512 * gg + 512, :].rearrange("(p t) k -> p t k", t=4),
            )

        ident = kept([P, P], F32, "ident")
        make_identity(nc, ident[:])

        arg = kept([P, 4], F32, "arg")
        nc.vector.tensor_scalar(
            out=arg[:], in0=lam_t[:], scalar1=4.0, scalar2=-4.0, op0=ALU.mult, op1=ALU.add
        )
        ex = kept([P, 4], F32, "ex")
        nc.scalar.activation(out=ex[:], in_=arg[:], func=ACT.Exp)
        den = kept([P, 4], F32, "den")
        nc.vector.tensor_scalar_add(den[:], ex[:], 1.0)
        h = kept([P, 4], F32, "h")
        nc.vector.reciprocal(h[:], den[:])
        hm = kept([P, 4], F32, "hm")
        nc.vector.tensor_scalar(out=hm[:], in0=h[:], scalar1=-1.0, scalar2=1.0, op0=ALU.mult, op1=ALU.add)
        a1 = kept([P, 4], F32, "a1")
        nc.vector.tensor_tensor(out=a1[:], in0=h[:], in1=g_t[:], op=ALU.mult)
        a2 = kept([P, 4], F32, "a2")
        nc.vector.tensor_tensor(out=a2[:], in0=hm[:], in1=g_t[:], op=ALU.mult)

        psi_grp = {}
        x_grp = {}
        psi_c, psi_s, x_c, x_s = {}, {}, {}, {}
        for b in range(2):
            for q in range(2):
                tag = "%d%d" % (b, q)
                psi_grp[b, q] = kept([P, 4, P, 4], BF16, "psi_grp_" + tag)
                x_grp[b, q] = keep.tile([P, N, 4], BF16, name="x_grp_" + tag, tag="columns", bufs=4, align_bytes=64)
                psi_c[b, q] = kept([P, K], U32, "psi_c_" + tag)
                psi_s[b, q] = kept([P, K], U8, "psi_s_" + tag)
                x_c[b, q] = kept([P, N], U32, "x_c_" + tag)
                x_s[b, q] = kept([P, N], U8, "x_s_" + tag)
        phi_grp, phi_c, phi_s = {}, {}, {}
        for gg in range(G):
            phi_grp[gg] = kept([P, 4, P, 4], BF16, "phi_grp_%d" % gg)
            phi_c[gg] = kept([P, K], U32, "phi_c_%d" % gg)
            phi_s[gg] = kept([P, K], U8, "phi_s_%d" % gg)
        part1 = kept([P, 4, N], F32, "part1")
        cg_flat, cg_grp, cg_c, cg_s = {}, {}, {}, {}
        for ch in CH:
            w = ch[1] - ch[0]
            cg_flat[ch] = kept([P, 4, w], BF16, "cg_flat_%d" % ch[0])
            cg_grp[ch] = kept([P, w, 4], BF16, "cg_grp_%d" % ch[0])
            cg_c[ch] = kept([P, w], U32, "cg_c_%d" % ch[0])
            cg_s[ch] = kept([P, w], U8, "cg_s_%d" % ch[0])
        out_s = kept([P, G, N], U8, "out_s")

        def copy(eng, dst, src):
            if eng == "v":
                nc.vector.tensor_copy(out=dst, in_=src)
            else:
                nc.scalar.copy(out=dst, in_=src)

        def quant(codes, scales, src):
            nc.vector.quantize_mx(out=codes.bitcast(FP8X4), scales=scales, in_=src)

        def interleave(eng, dst, src):
            copy(
                eng,
                dst.rearrange("p (c i) t -> p c t i", i=4),
                src.rearrange("p t (c i) -> p c t i", i=4),
            )

        def i_psi(eng, b, q, m0, m1):
            copy(
                eng,
                psi_grp[b, q][:, :, m0:m1, :].rearrange("p t m j -> p m j t"),
                psi_raw[b, q][:].rearrange("p j (m t) -> p m j t", t=4)[:, m0:m1],
            )

        def q_psi(b, q):
            quant(psi_c[b, q][:], psi_s[b, q][:], psi_grp[b, q][:].rearrange("p t m j -> p (t m j)"))

        def i_x(eng, b, q, a, z):
            interleave(eng, x_grp[b, q][:, a:z, :], x_raw[b, q][:, :, a:z])

        def q_x(b, q, a, z):
            quant(
                x_c[b, q][:, a:z],
                x_s[b, q][:, a:z],
                x_grp[b, q][:, a:z, :].rearrange("p n j -> p (n j)"),
            )

        def mm(dst, lc, ls, m, rc, rs, n0, n1, start, stop):
            nc.tensor.matmul_mx(
                out=dst,
                lhsT=lc[:, m : m + P].bitcast(FP8X4),
                lhsT_scale=ls[:, m : m + P],
                rhs=rc[:, n0:n1].bitcast(FP8X4),
                rhs_scale=rs[:, n0:n1],
                start=start,
                stop=stop,
            )

        bank = {}

        def mm1(b, ch, ts):
            w = ch[1] - ch[0]
            acc = psum.tile([P, len(ts), w], F32, name="acc1", tag="bank")
            bank[b, ch, ts] = acc
            for i in range(len(ts)):
                for q in range(2):
                    mm(
                        acc[:, i, :], psi_c[b, q], psi_s[b, q], P * ts[i],
                        x_c[b, q], x_s[b, q], ch[0], ch[1], q == 0, q == 1,
                    )

        def scale1(ch, ts):
            for i in range(len(ts)):
                t = ts[i]
                nc.scalar.activation(
                    out=part1[:, t, ch[0] : ch[1]], in_=bank[0, ch, ts][:, i, :],
                    func=ACT.Copy, scale=a1[:, t : t + 1],
                )

        def blend(ch, ts):
            for i in range(len(ts)):
                t = ts[i]
                nc.vector.scalar_tensor_tensor(
                    out=cg_flat[ch][:, t, :], in0=bank[1, ch, ts][:, i, :], scalar=a2[:, t : t + 1],
                    in1=part1[:, t, ch[0] : ch[1]], op0=ALU.mult, op1=ALU.add,
                )

        def i_cg(eng, c, a, z):
            interleave(eng, cg_grp[CH[c]][:, a:z, :], cg_flat[CH[c]][:, :, a:z])

        def q_cg(c):
            quant(cg_c[CH[c]][:], cg_s[CH[c]][:], cg_grp[CH[c]][:].rearrange("p n j -> p (n j)"))

        def t_phi(gg):
            words = phi_raw[gg][:].rearrange("p t k -> p (t k)").bitcast(F32)
            for half in range(2):
                acc = psum.tile([P, 2, 2, P], F32, name="acct", tag="bank")
                bank["phi", gg, half] = acc
                for a in range(2):
                    t = 2 * half + a
                    for u in range(2):
                        nc.tensor.transpose(acc[:, a, u, :], words[:, 256 * t + u : 256 * (t + 1) : 2], ident[:])

        def c_phi(eng, gg, half):
            dst = phi_grp[gg][:, 2 * half : 2 * half + 2].rearrange("p a m j -> p (a m j)").bitcast(F32)
            copy(
                eng,
                dst.rearrange("p (a m u) -> p a m u", a=2, u=2),
                bank["phi", gg, half][:].rearrange("p a u m -> p a m u"),
            )

        def q_phi(gg):
            quant(phi_c[gg][:], phi_s[gg][:], phi_grp[gg][:].rearrange("p t m j -> p (t m j)"))

        def xi(eng, b, q, c):
            i_x(eng, b, q, 256 * c, 256 * c + 256)

        def xq(b, q, c):
            q_x(b, q, CH[c][0], CH[c][1])

        SLOTS = (((0,), (1,), (2,), (3,)), ((0, 1), (2, 3)))

        def m1(b, c, h):
            mm1(b, CH[c], SLOTS[c][h])

        def sc(c, h):
            scale1(CH[c], SLOTS[c][h])

        def bl(c, h):
            blend(CH[c], SLOTS[c][h])

        out_f, out_b, out_c = {}, {}, {}

        def m2(gg, c, h):
            ts = SLOTS[c][h]
            w = CH[c][1] - CH[c][0]
            acc = psum.tile([P, len(ts), w], F32, name="acc2", tag="bank")
            bank["out", gg, c, h] = acc
            for i in range(len(ts)):
                mm(
                    acc[:, i, :], phi_c[gg], phi_s[gg], P * ts[i],
                    cg_c[CH[c]], cg_s[CH[c]], 0, w, True, True,
                )

        def A(eng, gg, c, h):
            if gg not in out_f:
                out_f[gg] = work.tile([P, 4, N], F32, name="out_f", bufs=3, align_bytes=64)
            ts = SLOTS[c][h]
            copy(
                eng,
                out_f[gg][:, ts[0] : ts[0] + len(ts), CH[c][0] : CH[c][1]],
                bank["out", gg, c, h][:],
            )

        def store_f(gg, t0, t1):
            nc.sync.dma_start(
                out=out_0[512 * gg : 512 * gg + 512, :].rearrange("(p t) n -> p t n", t=4)[:, t0:t1, :],
                in_=out_f[gg][:, t0:t1, :],
            )

        def B(eng, gg, c):
            if gg not in out_b:
                out_b[gg] = keep.tile([P, N, 4], BF16, name="out_b", tag="columns", bufs=4, align_bytes=64)
                out_c[gg] = work.tile([P, N], U32, name="out_c", bufs=3, align_bytes=64)
            a = 256 * c
            interleave(eng, out_b[gg][:, a : a + 256, :], out_f[gg][:, :, a : a + 256])

        def Q(gg, c):
            a, z = CH[c]
            quant(
                out_c[gg][:, a:z], out_s[:, gg, a:z],
                out_b[gg][:, a:z, :].rearrange("p n j -> p (n j)"),
            )

        def store_c(gg):
            nc.sync.dma_start(
                out=out_1[gg].rearrange("p n t -> p (n t)").bitcast(I32),
                in_=out_c[gg][:].bitcast(I32),
            )

        def store_s(queue, g0, g1):
            for quad in range(4):
                queue.dma_start(
                    out=out_2[g0:g1, 4 * quad : 4 * quad + 4, :].bitcast(I32).rearrange("g q n -> q g n"),
                    in_=out_s[32 * quad : 32 * quad + 4, g0:g1, :].bitcast(I32),
                )

        load_psi(0, 1)
        i_psi("s", 0, 1, 0, 64)
        i_psi("v", 0, 1, 64, 128)
        load_psi(0, 0)
        i_psi("v", 0, 0, 0, 64)
        load_x(0, 1)
        load_x(0, 0)
        load_psi(1, 0)
        q_psi(0, 1)
        i_psi("s", 0, 0, 64, 128)
        xi("s", 0, 1, 1)
        xi("v", 0, 1, 2)
        load_x(1, 0)
        load_x(1, 1)
        xi("v", 0, 1, 0)
        xi("s", 0, 0, 2)
        i_psi("s", 1, 0, 64, 128)
        xq(0, 1, 1)
        xq(0, 1, 0)
        xi("v", 0, 0, 1)
        xi("v", 0, 0, 0)
        xi("s", 1, 0, 1)
        xq(0, 0, 1)
        q_psi(0, 0)
        xq(0, 0, 0)
        xi("s", 1, 0, 0)
        m1(0, 0, 0)
        xi("v", 1, 0, 2)
        i_psi("v", 1, 0, 0, 64)
        xi("v", 1, 1, 1)
        m1(0, 0, 2)
        m1(0, 1, 1)
        xi("s", 1, 1, 0)
        load_psi(1, 1)
        i_psi("s", 1, 1, 0, 64)
        sc(0, 2)
        xq(1, 0, 1)
        load_phi(0)
        xq(1, 0, 0)
        sc(0, 0)
        m1(0, 0, 3)
        i_psi("v", 1, 1, 64, 128)
        sc(1, 1)
        t_phi(0)
        q_psi(1, 0)
        m1(0, 0, 1)
        xq(1, 1, 0)
        q_psi(1, 1)
        m1(1, 0, 2)
        load_phi(3)
        xi("v", 1, 1, 2)
        m1(1, 0, 0)
        bl(0, 2)
        c_phi("s", 0, 0)
        sc(0, 3)
        m1(1, 0, 3)
        bl(0, 0)
        sc(0, 1)
        m1(1, 0, 1)
        xq(1, 1, 1)
        c_phi("s", 0, 1)
        m1(0, 1, 0)
        bl(0, 3)
        bl(0, 1)
        load_phi(1)
        m1(1, 1, 1)
        bl(1, 1)
        sc(1, 0)
        m1(1, 1, 0)
        t_phi(3)
        bl(1, 0)
        q_phi(0)
        i_cg("s", 0, 0, 256)
        t_phi(1)
        i_cg("v", 1, 0, 256)
        i_cg("s", 0, 256, 512)
        c_phi("s", 3, 0)
        q_cg(1)
        q_cg(0)
        c_phi("s", 3, 1)
        c_phi("v", 1, 1)
        m2(0, 1, 1)
        q_phi(3)
        m2(0, 0, 2)
        A("v", 0, 0, 2)
        c_phi("s", 1, 0)
        m2(0, 0, 3)
        q_phi(1)
        A("s", 0, 1, 1)
        m2(3, 0, 3)
        m2(3, 0, 2)
        m2(3, 1, 1)
        A("s", 0, 0, 3)
        load_phi(2)
        A("s", 3, 0, 2)
        store_f(0, 2, 4)
        m2(3, 0, 0)
        A("s", 3, 0, 0)
        A("v", 3, 0, 3)
        m2(3, 0, 1)
        m2(1, 0, 2)
        m2(3, 1, 0)
        A("s", 1, 0, 2)
        m2(0, 0, 0)
        A("s", 0, 0, 0)
        A("v", 3, 1, 1)
        A("v", 3, 0, 1)
        A("v", 3, 1, 0)
        m2(1, 1, 1)
        A("s", 1, 1, 1)
        store_f(3, 2, 4)
        m2(1, 0, 3)
        B("v", 3, 1)
        m2(0, 1, 0)
        B("v", 3, 2)
        A("v", 0, 1, 0)
        t_phi(2)
        m2(1, 0, 1)
        A("s", 1, 0, 3)
        store_f(3, 0, 2)
        store_f(1, 2, 4)
        B("v", 3, 0)
        m2(0, 0, 1)
        A("v", 0, 0, 1)
        c_phi("s", 2, 0)
        c_phi("s", 2, 1)
        A("s", 1, 0, 1)
        m2(1, 1, 0)
        m2(1, 0, 0)
        A("s", 1, 1, 0)
        q_phi(2)
        m2(2, 1, 1)
        A("s", 1, 0, 0)
        B("v", 0, 1)
        store_f(0, 0, 2)
        B("s", 1, 2)
        m2(2, 0, 1)
        B("v", 0, 2)
        Q(3, 1)
        m2(2, 1, 0)
        A("s", 2, 1, 1)
        A("s", 2, 0, 1)
        m2(2, 0, 0)
        A("s", 2, 0, 0)
        B("v", 1, 0)
        m2(2, 0, 3)
        B("s", 0, 0)
        m2(2, 0, 2)
        Q(3, 0)
        store_f(1, 0, 2)
        A("v", 2, 0, 3)
        A("v", 2, 0, 2)
        Q(1, 1)
        B("v", 1, 1)
        B("v", 2, 1)
        A("s", 2, 1, 0)
        Q(1, 0)
        Q(0, 1)
        store_c(3)
        Q(0, 0)
        store_f(2, 2, 4)
        store_s(nc.scalar, 3, 4)
        store_f(2, 0, 2)
        store_c(0)
        B("s", 2, 0)
        B("v", 2, 2)
        Q(2, 0)
        store_c(1)
        Q(2, 1)
        store_s(nc.sync, 0, 3)
        store_c(2)
